import numpy as np
import ml_dtypes

BF16 = ml_dtypes.bfloat16


def bf(x):
    return np.asarray(x, np.float32).astype(BF16)


def f32(x):
    return np.asarray(x, np.float32)


def f64(x):
    return np.asarray(x).astype(np.float64)


def striped(idx):
    return np.tile(idx.reshape(-1, 16).T, (8, 1))


S, K, M, N, E, Q = 512, 512, 256, 256, 2, 128


def setup_inputs():
    return {"base": bf(np.random.standard_normal((M, S))), "x": bf(np.random.standard_normal((K, N))), "w": bf(np.random.standard_normal((E, K, M)) / np.sqrt(K)), "s": f32(0.5 + np.random.random_sample((M, 1))), "b": f32(0.5 * np.random.standard_normal((M, 1))), "offs": striped(np.random.permutation(S)[:N])}


def reference(base, x, w, s, b, offs):
    idx = offs[:16].T.reshape(-1)
    z = f64(base).copy()
    for e in range(E):
        z[:, idx[e * Q : (e + 1) * Q]] += f64(w)[e].T @ f64(x)[:, e * Q : (e + 1) * Q]
    return z * f64(s) + f64(b)

@@ -1,0 +1,70 @@
+import concourse.mybir as mybir
+from concourse.masks import make_identity
+
+BF16 = mybir.dt.bfloat16
+F32 = mybir.dt.float32
+U16 = mybir.dt.uint16
+MULT = mybir.AluOpType.mult
+ADD = mybir.AluOpType.add
+
+P = 128
+M = 256
+S = 512
+K = 512
+N = 256
+E = 2
+Q = N // E
+M_BLOCKS = M // P
+K_BLOCKS = K // P
+PIECE_COLUMNS = Q // 16
+
+FLOPS = 2 * M * K * N
+
+
+def tile_scatter_matmul_kernel(tc, base, x, w, s, b, offs, out):
+    nc = tc.nc
+    with (
+        tc.tile_pool(name="held", bufs=1) as held,
+        tc.psum_pool(name="banks", bufs=1) as banks,
+    ):
+        offsets = held.tile([P, N // 16], U16, name="offsets")
+        nc.sync.dma_start(offsets[:], offs)
+
+        base_tile = held.tile([P, M_BLOCKS, S], BF16, name="base_tile")
+        x_tile = held.tile([P, K_BLOCKS, N], BF16, name="x_tile")
+        w_tile = held.tile([P, E, K_BLOCKS, M], BF16, name="w_tile")
+        nc.sync.dma_start(base_tile[:], base.rearrange("(a p) t -> p a t", p=P))
+        nc.scalar.dma_start(x_tile[:], x.rearrange("(p c) j -> p c j", c=K_BLOCKS))
+        nc.scalar.dma_start(w_tile[:, 0], w[0].rearrange("(p c) m -> p c m", c=K_BLOCKS))
+        nc.sync.dma_start(w_tile[:, 1], w[1].rearrange("(p c) m -> p c m", c=K_BLOCKS))
+
+        identity = held.tile([P, P], BF16, name="identity")
+        make_identity(nc, identity[:])
+
+        gain = held.tile([P, M_BLOCKS], F32, name="gain")
+        shift = held.tile([P, M_BLOCKS], F32, name="shift")
+        nc.gpsimd.dma_start(gain[:], s.rearrange("(a p) o -> p (a o)", p=P))
+        nc.gpsimd.dma_start(shift[:], b.rearrange("(a p) o -> p (a o)", p=P))
+
+        windows = [banks.tile([P, S], F32, name=f"window{a}") for a in range(M_BLOCKS)]
+        for a in range(M_BLOCKS):
+            nc.tensor.matmul(windows[a][:], identity[:], base_tile[:, a], start=True, stop=False)
+
+        for a in range(M_BLOCKS):
+            for e in range(E):
+                piece = offsets[:, e * PIECE_COLUMNS : (e + 1) * PIECE_COLUMNS]
+                for c in range(K_BLOCKS):
+                    nc.tensor.matmul(
+                        windows[a][:].indirect(piece),
+                        w_tile[:, e, c, a * P : (a + 1) * P],
+                        x_tile[:, c, e * Q : (e + 1) * Q],
+                        start=False,
+                        stop=(e == E - 1 and c == K_BLOCKS - 1),
+                    )
+
+        for a in range(M_BLOCKS):
+            result = held.tile([P, S], F32, name=f"result{a}")
+            nc.vector.tensor_scalar(
+                result[:], windows[a][:], gain[:, a : a + 1], shift[:, a : a + 1], MULT, ADD
+            )
+            nc.sync.dma_start(out[a * P : (a + 1) * P, :], result[:])

@@ -17,6 +17,8 @@ Q = N // E
 M_BLOCKS = M // P
 K_BLOCKS = K // P
 PIECE_COLUMNS = Q // 16
+HALF = S // 2
+WARM_UP_MATMULS = 3
 
 FLOPS = 2 * M * K * N
 
@@ -28,23 +30,28 @@ def tile_scatter_matmul_kernel(tc, base, x, w, s, b, offs, out):
         tc.psum_pool(name="banks", bufs=1) as banks,
     ):
         offsets = held.tile([P, N // 16], U16, name="offsets")
-        nc.sync.dma_start(offsets[:], offs)
-
         base_tile = held.tile([P, M_BLOCKS, S], BF16, name="base_tile")
         x_tile = held.tile([P, K_BLOCKS, N], BF16, name="x_tile")
         w_tile = held.tile([P, E, K_BLOCKS, M], BF16, name="w_tile")
+        gain = held.tile([P, M_BLOCKS], F32, name="gain")
+        shift = held.tile([P, M_BLOCKS], F32, name="shift")
+
         nc.sync.dma_start(base_tile[:], base.rearrange("(a p) t -> p a t", p=P))
-        nc.scalar.dma_start(x_tile[:], x.rearrange("(p c) j -> p c j", c=K_BLOCKS))
-        nc.scalar.dma_start(w_tile[:, 0], w[0].rearrange("(p c) m -> p c m", c=K_BLOCKS))
-        nc.sync.dma_start(w_tile[:, 1], w[1].rearrange("(p c) m -> p c m", c=K_BLOCKS))
+        nc.sync.dma_start(offsets[:], offs)
+        nc.sync.dma_start(x_tile[:], x.rearrange("(p c) j -> p c j", c=K_BLOCKS))
+        for e in range(E):
+            nc.sync.dma_start(w_tile[:, e], w[e].rearrange("(p c) m -> p c m", c=K_BLOCKS))
+        nc.sync.dma_start(gain[:], s.rearrange("(a p) o -> p (a o)", p=P))
+        nc.sync.dma_start(shift[:], b.rearrange("(a p) o -> p (a o)", p=P))
+
+        zeros = held.tile([P, S], BF16, name="zeros")
+        nc.vector.memset(zeros[:], 0.0)
+        idle_bank = banks.tile([P, S], F32, name="idle_bank")
+        for i in range(WARM_UP_MATMULS):
+            nc.tensor.matmul(idle_bank[:], zeros[:, 0:P], zeros[:], start=True, stop=True)
 
         identity = held.tile([P, P], BF16, name="identity")
         make_identity(nc, identity[:])
-
-        gain = held.tile([P, M_BLOCKS], F32, name="gain")
-        shift = held.tile([P, M_BLOCKS], F32, name="shift")
-        nc.gpsimd.dma_start(gain[:], s.rearrange("(a p) o -> p (a o)", p=P))
-        nc.gpsimd.dma_start(shift[:], b.rearrange("(a p) o -> p (a o)", p=P))
 
         windows = [banks.tile([P, S], F32, name=f"window{a}") for a in range(M_BLOCKS)]
         for a in range(M_BLOCKS):
@@ -62,9 +69,17 @@ def tile_scatter_matmul_kernel(tc, base, x, w, s, b, offs, out):
                         stop=(e == E - 1 and c == K_BLOCKS - 1),
                     )
 
+        store_queues = [nc.sync, nc.scalar]
         for a in range(M_BLOCKS):
             result = held.tile([P, S], F32, name=f"result{a}")
-            nc.vector.tensor_scalar(
-                result[:], windows[a][:], gain[:, a : a + 1], shift[:, a : a + 1], MULT, ADD
-            )
-            nc.sync.dma_start(out[a * P : (a + 1) * P, :], result[:])
+            for h in range(2):
+                columns = slice(h * HALF, (h + 1) * HALF)
+                nc.vector.tensor_scalar(
+                    result[:, columns],
+                    windows[a][:, columns],
+                    gain[:, a : a + 1],
+                    shift[:, a : a + 1],
+                    MULT,
+                    ADD,
+                )
+                store_queues[h].dma_start(out[a * P : (a + 1) * P, columns], result[:, columns])

@@ -16,6 +16,8 @@ E = 2
 Q = N // E
 M_BLOCKS = M // P
 K_BLOCKS = K // P
+K_PARTS = 2
+PART_BLOCKS = K_BLOCKS // K_PARTS
 PIECE_COLUMNS = Q // 16
 HALF = S // 2
 WARM_UP_MATMULS = 3
@@ -31,16 +33,25 @@ def tile_scatter_matmul_kernel(tc, base, x, w, s, b, offs, out):
     ):
         offsets = held.tile([P, N // 16], U16, name="offsets")
         base_tile = held.tile([P, M_BLOCKS, S], BF16, name="base_tile")
-        x_tile = held.tile([P, K_BLOCKS, N], BF16, name="x_tile")
-        w_tile = held.tile([P, E, K_BLOCKS, M], BF16, name="w_tile")
+        x_parts = [held.tile([P, PART_BLOCKS, N], BF16, name=f"x_part{r}") for r in range(K_PARTS)]
+        w_parts = [
+            [held.tile([P, PART_BLOCKS, M], BF16, name=f"w_part{e}_{r}") for r in range(K_PARTS)]
+            for e in range(E)
+        ]
         gain = held.tile([P, M_BLOCKS], F32, name="gain")
         shift = held.tile([P, M_BLOCKS], F32, name="shift")
 
+        x_blocks = x.rearrange("(p c) j -> p c j", c=K_BLOCKS)
+        w_blocks = w.rearrange("e (p c) m -> e p c m", c=K_BLOCKS)
+
         nc.sync.dma_start(base_tile[:], base.rearrange("(a p) t -> p a t", p=P))
         nc.sync.dma_start(offsets[:], offs)
-        nc.sync.dma_start(x_tile[:], x.rearrange("(p c) j -> p c j", c=K_BLOCKS))
         for e in range(E):
-            nc.sync.dma_start(w_tile[:, e], w[e].rearrange("(p c) m -> p c m", c=K_BLOCKS))
+            for r in range(K_PARTS):
+                blocks = slice(r * PART_BLOCKS, (r + 1) * PART_BLOCKS)
+                if e == 0:
+                    nc.sync.dma_start(x_parts[r][:], x_blocks[:, blocks])
+                nc.sync.dma_start(w_parts[e][r][:], w_blocks[e][:, blocks])
         nc.sync.dma_start(gain[:], s.rearrange("(a p) o -> p (a o)", p=P))
         nc.sync.dma_start(shift[:], b.rearrange("(a p) o -> p (a o)", p=P))
 
@@ -57,17 +68,24 @@ def tile_scatter_matmul_kernel(tc, base, x, w, s, b, offs, out):
         for a in range(M_BLOCKS):
             nc.tensor.matmul(windows[a][:], identity[:], base_tile[:, a], start=True, stop=False)
 
+        def scatter_part(a, e, r, closes):
+            piece = offsets[:, e * PIECE_COLUMNS : (e + 1) * PIECE_COLUMNS]
+            for c in range(PART_BLOCKS):
+                nc.tensor.matmul(
+                    windows[a][:].indirect(piece),
+                    w_parts[e][r][:, c, a * P : (a + 1) * P],
+                    x_parts[r][:, c, e * Q : (e + 1) * Q],
+                    start=False,
+                    stop=(closes and c == PART_BLOCKS - 1),
+                )
+
+        for e in range(E - 1):
+            for r in range(K_PARTS):
+                for a in range(M_BLOCKS):
+                    scatter_part(a, e, r, closes=False)
         for a in range(M_BLOCKS):
-            for e in range(E):
-                piece = offsets[:, e * PIECE_COLUMNS : (e + 1) * PIECE_COLUMNS]
-                for c in range(K_BLOCKS):
-                    nc.tensor.matmul(
-                        windows[a][:].indirect(piece),
-                        w_tile[:, e, c, a * P : (a + 1) * P],
-                        x_tile[:, c, e * Q : (e + 1) * Q],
-                        start=False,
-                        stop=(e == E - 1 and c == K_BLOCKS - 1),
-                    )
+            for r in range(K_PARTS):
+                scatter_part(a, E - 1, r, closes=(r == K_PARTS - 1))
 
         store_queues = [nc.sync, nc.scalar]
         for a in range(M_BLOCKS):

@@ -20,7 +20,6 @@ K_PARTS = 2
 PART_BLOCKS = K_BLOCKS // K_PARTS
 PIECE_COLUMNS = Q // 16
 HALF = S // 2
-WARM_UP_MATMULS = 3
 
 FLOPS = 2 * M * K * N
 
@@ -54,12 +53,6 @@ def tile_scatter_matmul_kernel(tc, base, x, w, s, b, offs, out):
                 nc.sync.dma_start(w_parts[e][r][:], w_blocks[e][:, blocks])
         nc.sync.dma_start(gain[:], s.rearrange("(a p) o -> p (a o)", p=P))
         nc.sync.dma_start(shift[:], b.rearrange("(a p) o -> p (a o)", p=P))
-
-        zeros = held.tile([P, S], BF16, name="zeros")
-        nc.vector.memset(zeros[:], 0.0)
-        idle_bank = banks.tile([P, S], F32, name="idle_bank")
-        for i in range(WARM_UP_MATMULS):
-            nc.tensor.matmul(idle_bank[:], zeros[:, 0:P], zeros[:], start=True, stop=True)
 
         identity = held.tile([P, P], BF16, name="identity")
         make_identity(nc, identity[:])

@@ -20,6 +20,7 @@ K_PARTS = 2
 PART_BLOCKS = K_BLOCKS // K_PARTS
 PIECE_COLUMNS = Q // 16
 HALF = S // 2
+WARM_UP_MATMULS = 3
 
 FLOPS = 2 * M * K * N
 
@@ -45,14 +46,19 @@ def tile_scatter_matmul_kernel(tc, base, x, w, s, b, offs, out):
 
         nc.sync.dma_start(base_tile[:], base.rearrange("(a p) t -> p a t", p=P))
         nc.sync.dma_start(offsets[:], offs)
-        for e in range(E):
-            for r in range(K_PARTS):
-                blocks = slice(r * PART_BLOCKS, (r + 1) * PART_BLOCKS)
-                if e == 0:
-                    nc.sync.dma_start(x_parts[r][:], x_blocks[:, blocks])
+        for r in range(K_PARTS):
+            blocks = slice(r * PART_BLOCKS, (r + 1) * PART_BLOCKS)
+            nc.sync.dma_start(x_parts[r][:], x_blocks[:, blocks])
+            for e in range(E):
                 nc.sync.dma_start(w_parts[e][r][:], w_blocks[e][:, blocks])
         nc.sync.dma_start(gain[:], s.rearrange("(a p) o -> p (a o)", p=P))
         nc.sync.dma_start(shift[:], b.rearrange("(a p) o -> p (a o)", p=P))
+
+        zeros = held.tile([P, S], BF16, name="zeros")
+        nc.vector.memset(zeros[:], 0.0)
+        idle_bank = banks.tile([P, S], F32, name="idle_bank")
+        for i in range(WARM_UP_MATMULS):
+            nc.tensor.matmul(idle_bank[:], zeros[:, 0:P], zeros[:], start=True, stop=True)
 
         identity = held.tile([P, P], BF16, name="identity")
         make_identity(nc, identity[:])
@@ -72,13 +78,13 @@ def tile_scatter_matmul_kernel(tc, base, x, w, s, b, offs, out):
                     stop=(closes and c == PART_BLOCKS - 1),
                 )
 
-        for e in range(E - 1):
-            for r in range(K_PARTS):
+        for r in range(K_PARTS - 1):
+            for e in range(E):
                 for a in range(M_BLOCKS):
                     scatter_part(a, e, r, closes=False)
         for a in range(M_BLOCKS):
-            for r in range(K_PARTS):
-                scatter_part(a, E - 1, r, closes=(r == K_PARTS - 1))
+            for e in range(E):
+                scatter_part(a, e, K_PARTS - 1, closes=(e == E - 1))
 
         store_queues = [nc.sync, nc.scalar]
         for a in range(M_BLOCKS):

@@ -19,7 +19,7 @@ K_BLOCKS = K // P
 K_PARTS = 2
 PART_BLOCKS = K_BLOCKS // K_PARTS
 PIECE_COLUMNS = Q // 16
-HALF = S // 2
+PIECE_WIDTHS = [S // 2, S // 4, S // 4]
 WARM_UP_MATMULS = 3
 
 FLOPS = 2 * M * K * N
@@ -89,8 +89,9 @@ def tile_scatter_matmul_kernel(tc, base, x, w, s, b, offs, out):
         store_queues = [nc.sync, nc.scalar]
         for a in range(M_BLOCKS):
             result = held.tile([P, S], F32, name=f"result{a}")
-            for h in range(2):
-                columns = slice(h * HALF, (h + 1) * HALF)
+            first = 0
+            for i, width in enumerate(PIECE_WIDTHS):
+                columns = slice(first, first + width)
                 nc.vector.tensor_scalar(
                     result[:, columns],
                     windows[a][:, columns],
@@ -99,4 +100,5 @@ def tile_scatter_matmul_kernel(tc, base, x, w, s, b, offs, out):
                     MULT,
                     ADD,
                 )
-                store_queues[h].dma_start(out[a * P : (a + 1) * P, columns], result[:, columns])
+                store_queues[i % 2].dma_start(out[a * P : (a + 1) * P, columns], result[:, columns])
+                first += width

@@ -16,11 +16,11 @@ E = 2
 Q = N // E
 M_BLOCKS = M // P
 K_BLOCKS = K // P
-K_PARTS = 2
-PART_BLOCKS = K_BLOCKS // K_PARTS
+PART_BLOCKS = [1, 1, 2]
 PIECE_COLUMNS = Q // 16
-PIECE_WIDTHS = [S // 2, S // 4, S // 4]
-WARM_UP_MATMULS = 3
+PIECE_WIDTHS = [S // 2, S // 2]
+LAST_PIECE_WIDTHS = [S // 2, S // 4, S // 4]
+WARM_UP_MATMULS = 16
 
 FLOPS = 2 * M * K * N
 
@@ -31,37 +31,44 @@ def tile_scatter_matmul_kernel(tc, base, x, w, s, b, offs, out):
         tc.tile_pool(name="held", bufs=1) as held,
         tc.psum_pool(name="banks", bufs=1) as banks,
     ):
-        offsets = held.tile([P, N // 16], U16, name="offsets")
-        base_tile = held.tile([P, M_BLOCKS, S], BF16, name="base_tile")
-        x_parts = [held.tile([P, PART_BLOCKS, N], BF16, name=f"x_part{r}") for r in range(K_PARTS)]
-        w_parts = [
-            [held.tile([P, PART_BLOCKS, M], BF16, name=f"w_part{e}_{r}") for r in range(K_PARTS)]
-            for e in range(E)
-        ]
-        gain = held.tile([P, M_BLOCKS], F32, name="gain")
-        shift = held.tile([P, M_BLOCKS], F32, name="shift")
-
-        x_blocks = x.rearrange("(p c) j -> p c j", c=K_BLOCKS)
-        w_blocks = w.rearrange("e (p c) m -> e p c m", c=K_BLOCKS)
-
-        nc.sync.dma_start(base_tile[:], base.rearrange("(a p) t -> p a t", p=P))
-        nc.sync.dma_start(offsets[:], offs)
-        for r in range(K_PARTS):
-            blocks = slice(r * PART_BLOCKS, (r + 1) * PART_BLOCKS)
-            nc.sync.dma_start(x_parts[r][:], x_blocks[:, blocks])
-            for e in range(E):
-                nc.sync.dma_start(w_parts[e][r][:], w_blocks[e][:, blocks])
-        nc.sync.dma_start(gain[:], s.rearrange("(a p) o -> p (a o)", p=P))
-        nc.sync.dma_start(shift[:], b.rearrange("(a p) o -> p (a o)", p=P))
-
-        zeros = held.tile([P, S], BF16, name="zeros")
-        nc.vector.memset(zeros[:], 0.0)
-        idle_bank = banks.tile([P, S], F32, name="idle_bank")
+        zeros = held.tile([P, P], BF16, name="zeros")
+        nc.gpsimd.memset(zeros[:], 0.0)
+        idle_bank = banks.tile([P, P], F32, name="idle_bank")
         for i in range(WARM_UP_MATMULS):
-            nc.tensor.matmul(idle_bank[:], zeros[:, 0:P], zeros[:], start=True, stop=True)
+            nc.tensor.matmul(idle_bank[:], zeros[:], zeros[:], start=True, stop=True)
 
         identity = held.tile([P, P], BF16, name="identity")
         make_identity(nc, identity[:])
+
+        x_blocks = x.rearrange("(p c) j -> p c j", c=K_BLOCKS)
+        w_blocks = w.rearrange("e (p c) m -> p e c m", c=K_BLOCKS)
+
+        base_tile = held.tile([P, M_BLOCKS, S], BF16, name="base_tile")
+        nc.sync.dma_start(base_tile[:], base.rearrange("(a p) t -> p a t", p=P))
+        offsets = held.tile([P, N // 16], U16, name="offsets")
+        nc.sync.dma_start(offsets[:], offs)
+        x_parts = []
+        w_parts = []
+        first_block = 0
+        for r, count in enumerate(PART_BLOCKS):
+            blocks = slice(first_block, first_block + count)
+            x_part = held.tile([P, count, N], BF16, name=f"x_part{r}")
+            nc.sync.dma_start(x_part[:], x_blocks[:, blocks])
+            x_parts.append(x_part)
+            if count == 1:
+                both = held.tile([P, E, count, M], BF16, name=f"w_part{r}")
+                nc.sync.dma_start(both[:], w_blocks[:, :, blocks])
+                w_parts.append([both[:, e] for e in range(E)])
+            else:
+                each = [held.tile([P, count, M], BF16, name=f"w_part{r}_{e}") for e in range(E)]
+                for e in range(E):
+                    nc.sync.dma_start(each[e][:], w_blocks[:, e, blocks])
+                w_parts.append([each[e][:] for e in range(E)])
+            first_block += count
+        gain = held.tile([P, M_BLOCKS], F32, name="gain")
+        shift = held.tile([P, M_BLOCKS], F32, name="shift")
+        nc.sync.dma_start(gain[:], s.rearrange("(a p) o -> p (a o)", p=P))
+        nc.sync.dma_start(shift[:], b.rearrange("(a p) o -> p (a o)", p=P))
 
         windows = [banks.tile([P, S], F32, name=f"window{a}") for a in range(M_BLOCKS)]
         for a in range(M_BLOCKS):
@@ -69,28 +76,29 @@ def tile_scatter_matmul_kernel(tc, base, x, w, s, b, offs, out):
 
         def scatter_part(a, e, r, closes):
             piece = offsets[:, e * PIECE_COLUMNS : (e + 1) * PIECE_COLUMNS]
-            for c in range(PART_BLOCKS):
+            for c in range(PART_BLOCKS[r]):
                 nc.tensor.matmul(
                     windows[a][:].indirect(piece),
-                    w_parts[e][r][:, c, a * P : (a + 1) * P],
+                    w_parts[r][e][:, c, a * P : (a + 1) * P],
                     x_parts[r][:, c, e * Q : (e + 1) * Q],
                     start=False,
-                    stop=(closes and c == PART_BLOCKS - 1),
+                    stop=(closes and c == PART_BLOCKS[r] - 1),
                 )
 
-        for r in range(K_PARTS - 1):
+        last_part = len(PART_BLOCKS) - 1
+        for r in range(last_part):
             for e in range(E):
                 for a in range(M_BLOCKS):
                     scatter_part(a, e, r, closes=False)
         for a in range(M_BLOCKS):
             for e in range(E):
-                scatter_part(a, e, K_PARTS - 1, closes=(e == E - 1))
+                scatter_part(a, e, last_part, closes=(e == E - 1))
 
         store_queues = [nc.sync, nc.scalar]
         for a in range(M_BLOCKS):
             result = held.tile([P, S], F32, name=f"result{a}")
             first = 0
-            for i, width in enumerate(PIECE_WIDTHS):
+            for i, width in enumerate(LAST_PIECE_WIDTHS if a == M_BLOCKS - 1 else PIECE_WIDTHS):
                 columns = slice(first, first + width)
                 nc.vector.tensor_scalar(
                     result[:, columns],

@@ -18,9 +18,8 @@ M_BLOCKS = M // P
 K_BLOCKS = K // P
 PART_BLOCKS = [1, 1, 2]
 PIECE_COLUMNS = Q // 16
-PIECE_WIDTHS = [S // 2, S // 2]
-LAST_PIECE_WIDTHS = [S // 2, S // 4, S // 4]
-WARM_UP_MATMULS = 16
+PIECES = 2
+WARM_UP_MATMULS = 12
 
 FLOPS = 2 * M * K * N
 
@@ -43,8 +42,9 @@ def tile_scatter_matmul_kernel(tc, base, x, w, s, b, offs, out):
         x_blocks = x.rearrange("(p c) j -> p c j", c=K_BLOCKS)
         w_blocks = w.rearrange("e (p c) m -> p e c m", c=K_BLOCKS)
 
-        base_tile = held.tile([P, M_BLOCKS, S], BF16, name="base_tile")
-        nc.sync.dma_start(base_tile[:], base.rearrange("(a p) t -> p a t", p=P))
+        base_tiles = [held.tile([P, S], BF16, name=f"base_tile{a}") for a in range(M_BLOCKS)]
+        for a in range(M_BLOCKS):
+            nc.sync.dma_start(base_tiles[a][:], base[a * P : (a + 1) * P, :])
         offsets = held.tile([P, N // 16], U16, name="offsets")
         nc.sync.dma_start(offsets[:], offs)
         x_parts = []
@@ -72,7 +72,7 @@ def tile_scatter_matmul_kernel(tc, base, x, w, s, b, offs, out):
 
         windows = [banks.tile([P, S], F32, name=f"window{a}") for a in range(M_BLOCKS)]
         for a in range(M_BLOCKS):
-            nc.tensor.matmul(windows[a][:], identity[:], base_tile[:, a], start=True, stop=False)
+            nc.tensor.matmul(windows[a][:], identity[:], base_tiles[a][:], start=True, stop=False)
 
         def scatter_part(a, e, r, closes):
             piece = offsets[:, e * PIECE_COLUMNS : (e + 1) * PIECE_COLUMNS]
@@ -97,9 +97,8 @@ def tile_scatter_matmul_kernel(tc, base, x, w, s, b, offs, out):
         store_queues = [nc.sync, nc.scalar]
         for a in range(M_BLOCKS):
             result = held.tile([P, S], F32, name=f"result{a}")
-            first = 0
-            for i, width in enumerate(LAST_PIECE_WIDTHS if a == M_BLOCKS - 1 else PIECE_WIDTHS):
-                columns = slice(first, first + width)
+            for i in range(PIECES):
+                columns = slice(i * (S // PIECES), (i + 1) * (S // PIECES))
                 nc.vector.tensor_scalar(
                     result[:, columns],
                     windows[a][:, columns],
@@ -109,4 +108,3 @@ def tile_scatter_matmul_kernel(tc, base, x, w, s, b, offs, out):
                     ADD,
                 )
                 store_queues[i % 2].dma_start(out[a * P : (a + 1) * P, columns], result[:, columns])
-                first += width

@@ -17,6 +17,7 @@ Q = N // E
 M_BLOCKS = M // P
 K_BLOCKS = K // P
 PART_BLOCKS = [1, 1, 2]
+X_PART_BLOCKS = 2
 PIECE_COLUMNS = Q // 16
 PIECES = 2
 WARM_UP_MATMULS = 12
@@ -47,15 +48,17 @@ def tile_scatter_matmul_kernel(tc, base, x, w, s, b, offs, out):
             nc.sync.dma_start(base_tiles[a][:], base[a * P : (a + 1) * P, :])
         offsets = held.tile([P, N // 16], U16, name="offsets")
         nc.sync.dma_start(offsets[:], offs)
-        x_parts = []
+        x_halves = []
         w_parts = []
+        first_blocks = []
         first_block = 0
         for r, count in enumerate(PART_BLOCKS):
             blocks = slice(first_block, first_block + count)
-            x_part = held.tile([P, count, N], BF16, name=f"x_part{r}")
-            nc.sync.dma_start(x_part[:], x_blocks[:, blocks])
-            x_parts.append(x_part)
-            if count == 1:
+            if first_block % X_PART_BLOCKS == 0:
+                x_half = held.tile([P, X_PART_BLOCKS, N], BF16, name=f"x_half{len(x_halves)}")
+                nc.sync.dma_start(x_half[:], x_blocks[:, first_block : first_block + X_PART_BLOCKS])
+                x_halves.append(x_half)
+            if r == 1:
                 both = held.tile([P, E, count, M], BF16, name=f"w_part{r}")
                 nc.sync.dma_start(both[:], w_blocks[:, :, blocks])
                 w_parts.append([both[:, e] for e in range(E)])
@@ -64,6 +67,7 @@ def tile_scatter_matmul_kernel(tc, base, x, w, s, b, offs, out):
                 for e in range(E):
                     nc.sync.dma_start(each[e][:], w_blocks[:, e, blocks])
                 w_parts.append([each[e][:] for e in range(E)])
+            first_blocks.append(first_block)
             first_block += count
         gain = held.tile([P, M_BLOCKS], F32, name="gain")
         shift = held.tile([P, M_BLOCKS], F32, name="shift")
@@ -77,10 +81,11 @@ def tile_scatter_matmul_kernel(tc, base, x, w, s, b, offs, out):
         def scatter_part(a, e, r, closes):
             piece = offsets[:, e * PIECE_COLUMNS : (e + 1) * PIECE_COLUMNS]
             for c in range(PART_BLOCKS[r]):
+                block = first_blocks[r] + c
                 nc.tensor.matmul(
                     windows[a][:].indirect(piece),
                     w_parts[r][e][:, c, a * P : (a + 1) * P],
-                    x_parts[r][:, c, e * Q : (e + 1) * Q],
+                    x_halves[block // X_PART_BLOCKS][:, block % X_PART_BLOCKS, e * Q : (e + 1) * Q],
                     start=False,
                     stop=(closes and c == PART_BLOCKS[r] - 1),
                 )

@@ -99,7 +99,7 @@ def tile_scatter_matmul_kernel(tc, base, x, w, s, b, offs, out):
             for e in range(E):
                 scatter_part(a, e, last_part, closes=(e == E - 1))
 
-        store_queues = [nc.sync, nc.scalar]
+        store_queues = [nc.scalar, nc.sync]
         for a in range(M_BLOCKS):
             result = held.tile([P, S], F32, name=f"result{a}")
             for i in range(PIECES):

@@ -16,8 +16,6 @@ E = 2
 Q = N // E
 M_BLOCKS = M // P
 K_BLOCKS = K // P
-PART_BLOCKS = [1, 1, 2]
-X_PART_BLOCKS = 2
 PIECE_COLUMNS = Q // 16
 PIECES = 2
 WARM_UP_MATMULS = 12
@@ -48,27 +46,30 @@ def tile_scatter_matmul_kernel(tc, base, x, w, s, b, offs, out):
             nc.sync.dma_start(base_tiles[a][:], base[a * P : (a + 1) * P, :])
         offsets = held.tile([P, N // 16], U16, name="offsets")
         nc.sync.dma_start(offsets[:], offs)
-        x_halves = []
-        w_parts = []
-        first_blocks = []
-        first_block = 0
-        for r, count in enumerate(PART_BLOCKS):
-            blocks = slice(first_block, first_block + count)
-            if first_block % X_PART_BLOCKS == 0:
-                x_half = held.tile([P, X_PART_BLOCKS, N], BF16, name=f"x_half{len(x_halves)}")
-                nc.sync.dma_start(x_half[:], x_blocks[:, first_block : first_block + X_PART_BLOCKS])
-                x_halves.append(x_half)
-            if r == 1:
-                both = held.tile([P, E, count, M], BF16, name=f"w_part{r}")
-                nc.sync.dma_start(both[:], w_blocks[:, :, blocks])
-                w_parts.append([both[:, e] for e in range(E)])
-            else:
-                each = [held.tile([P, count, M], BF16, name=f"w_part{r}_{e}") for e in range(E)]
-                for e in range(E):
-                    nc.sync.dma_start(each[e][:], w_blocks[:, e, blocks])
-                w_parts.append([each[e][:] for e in range(E)])
-            first_blocks.append(first_block)
-            first_block += count
+
+        x_block = {}
+        w_block = {}
+
+        def load_x(first, count):
+            part = held.tile([P, count, N], BF16, name=f"x_part{first}")
+            nc.sync.dma_start(part[:], x_blocks[:, first : first + count])
+            for c in range(count):
+                x_block[first + c] = part[:, c]
+
+        def load_w(e, first, count):
+            part = held.tile([P, count, M], BF16, name=f"w_part{e}_{first}")
+            nc.sync.dma_start(part[:], w_blocks[:, e, first : first + count])
+            for c in range(count):
+                w_block[e, first + c] = part[:, c]
+
+        load_x(0, 1)
+        load_w(0, 0, 1)
+        load_w(1, 0, 2)
+        load_x(1, 1)
+        load_w(0, 1, 3)
+        load_x(2, 2)
+        load_w(1, 2, 2)
+
         gain = held.tile([P, M_BLOCKS], F32, name="gain")
         shift = held.tile([P, M_BLOCKS], F32, name="shift")
         nc.sync.dma_start(gain[:], s.rearrange("(a p) o -> p (a o)", p=P))
@@ -78,26 +79,22 @@ def tile_scatter_matmul_kernel(tc, base, x, w, s, b, offs, out):
         for a in range(M_BLOCKS):
             nc.tensor.matmul(windows[a][:], identity[:], base_tiles[a][:], start=True, stop=False)
 
-        def scatter_part(a, e, r, closes):
-            piece = offsets[:, e * PIECE_COLUMNS : (e + 1) * PIECE_COLUMNS]
-            for c in range(PART_BLOCKS[r]):
-                block = first_blocks[r] + c
-                nc.tensor.matmul(
-                    windows[a][:].indirect(piece),
-                    w_parts[r][e][:, c, a * P : (a + 1) * P],
-                    x_halves[block // X_PART_BLOCKS][:, block % X_PART_BLOCKS, e * Q : (e + 1) * Q],
-                    start=False,
-                    stop=(closes and c == PART_BLOCKS[r] - 1),
-                )
+        def scatter(a, e, c, closes):
+            nc.tensor.matmul(
+                windows[a][:].indirect(offsets[:, e * PIECE_COLUMNS : (e + 1) * PIECE_COLUMNS]),
+                w_block[e, c][:, a * P : (a + 1) * P],
+                x_block[c][:, e * Q : (e + 1) * Q],
+                start=False,
+                stop=closes,
+            )
 
-        last_part = len(PART_BLOCKS) - 1
-        for r in range(last_part):
-            for e in range(E):
-                for a in range(M_BLOCKS):
-                    scatter_part(a, e, r, closes=False)
+        for e, c in [(0, 0), (1, 0), (1, 1), (0, 1)]:
+            for a in range(M_BLOCKS):
+                scatter(a, e, c, closes=False)
         for a in range(M_BLOCKS):
             for e in range(E):
-                scatter_part(a, e, last_part, closes=(e == E - 1))
+                for c in range(2, K_BLOCKS):
+                    scatter(a, e, c, closes=(e == E - 1 and c == K_BLOCKS - 1))
 
         store_queues = [nc.scalar, nc.sync]
         for a in range(M_BLOCKS):

@@ -96,7 +96,6 @@ def tile_scatter_matmul_kernel(tc, base, x, w, s, b, offs, out):
                 for c in range(2, K_BLOCKS):
                     scatter(a, e, c, closes=(e == E - 1 and c == K_BLOCKS - 1))
 
-        store_queues = [nc.scalar, nc.sync]
         for a in range(M_BLOCKS):
             result = held.tile([P, S], F32, name=f"result{a}")
             for i in range(PIECES):
@@ -109,4 +108,4 @@ def tile_scatter_matmul_kernel(tc, base, x, w, s, b, offs, out):
                     MULT,
                     ADD,
                 )
-                store_queues[i % 2].dma_start(out[a * P : (a + 1) * P, columns], result[:, columns])
+                nc.sync.dma_start(out[a * P : (a + 1) * P, columns], result[:, columns])

@@ -29,11 +29,12 @@ def tile_scatter_matmul_kernel(tc, base, x, w, s, b, offs, out):
         tc.tile_pool(name="held", bufs=1) as held,
         tc.psum_pool(name="banks", bufs=1) as banks,
     ):
-        zeros = held.tile([P, P], BF16, name="zeros")
-        nc.gpsimd.memset(zeros[:], 0.0)
+        zero = held.tile([P, 1], BF16, name="zero")
+        nc.gpsimd.memset(zero[:], 0.0)
+        zeros = zero[:].to_broadcast([P, P])
         idle_bank = banks.tile([P, P], F32, name="idle_bank")
         for i in range(WARM_UP_MATMULS):
-            nc.tensor.matmul(idle_bank[:], zeros[:], zeros[:], start=True, stop=True)
+            nc.tensor.matmul(idle_bank[:], zeros, zeros, start=True, stop=True)
 
         identity = held.tile([P, P], BF16, name="identity")
         make_identity(nc, identity[:])

@@ -37,7 +37,8 @@ def tile_scatter_matmul_kernel(tc, base, x, w, s, b, offs, out):
             nc.tensor.matmul(idle_bank[:], zeros, zeros, start=True, stop=True)
 
         identity = held.tile([P, P], BF16, name="identity")
-        make_identity(nc, identity[:])
+        nc.vector.memset(identity[:], 0.0)
+        make_identity(nc, identity[:], nomemset=True)
 
         x_blocks = x.rearrange("(p c) j -> p c j", c=K_BLOCKS)
         w_blocks = w.rearrange("e (p c) m -> p e c m", c=K_BLOCKS)

@@ -17,6 +17,7 @@ Q = N // E
 M_BLOCKS = M // P
 K_BLOCKS = K // P
 PIECE_COLUMNS = Q // 16
+ROW_START = 256
 PIECES = 2
 WARM_UP_MATMULS = 12
 
@@ -43,7 +44,9 @@ def tile_scatter_matmul_kernel(tc, base, x, w, s, b, offs, out):
         x_blocks = x.rearrange("(p c) j -> p c j", c=K_BLOCKS)
         w_blocks = w.rearrange("e (p c) m -> p e c m", c=K_BLOCKS)
 
-        base_tiles = [held.tile([P, S], BF16, name=f"base_tile{a}") for a in range(M_BLOCKS)]
+        base_tiles = [
+            held.tile([P, S], BF16, name=f"base_tile{a}", align_bytes=ROW_START) for a in range(M_BLOCKS)
+        ]
         for a in range(M_BLOCKS):
             nc.sync.dma_start(base_tiles[a][:], base[a * P : (a + 1) * P, :])
         offsets = held.tile([P, N // 16], U16, name="offsets")
@@ -53,13 +56,13 @@ def tile_scatter_matmul_kernel(tc, base, x, w, s, b, offs, out):
         w_block = {}
 
         def load_x(first, count):
-            part = held.tile([P, count, N], BF16, name=f"x_part{first}")
+            part = held.tile([P, count, N], BF16, name=f"x_part{first}", align_bytes=ROW_START)
             nc.sync.dma_start(part[:], x_blocks[:, first : first + count])
             for c in range(count):
                 x_block[first + c] = part[:, c]
 
         def load_w(e, first, count):
-            part = held.tile([P, count, M], BF16, name=f"w_part{e}_{first}")
+            part = held.tile([P, count, M], BF16, name=f"w_part{e}_{first}", align_bytes=ROW_START)
             nc.sync.dma_start(part[:], w_blocks[:, e, first : first + count])
             for c in range(count):
                 w_block[e, first + c] = part[:, c]
@@ -99,7 +102,7 @@ def tile_scatter_matmul_kernel(tc, base, x, w, s, b, offs, out):
                     scatter(a, e, c, closes=(e == E - 1 and c == K_BLOCKS - 1))
 
         for a in range(M_BLOCKS):
-            result = held.tile([P, S], F32, name=f"result{a}")
+            result = held.tile([P, S], F32, name=f"result{a}", align_bytes=ROW_START)
             for i in range(PIECES):
                 columns = slice(i * (S // PIECES), (i + 1) * (S // PIECES))
                 nc.vector.tensor_scalar(

@@ -19,7 +19,7 @@ K_BLOCKS = K // P
 PIECE_COLUMNS = Q // 16
 ROW_START = 256
 PIECES = 2
-WARM_UP_MATMULS = 12
+WARM_UP_MATMULS = 3
 
 FLOPS = 2 * M * K * N
 
@@ -32,10 +32,11 @@ def tile_scatter_matmul_kernel(tc, base, x, w, s, b, offs, out):
     ):
         zero = held.tile([P, 1], BF16, name="zero")
         nc.gpsimd.memset(zero[:], 0.0)
-        zeros = zero[:].to_broadcast([P, P])
-        idle_bank = banks.tile([P, P], F32, name="idle_bank")
+        idle_bank = banks.tile([P, S], F32, name="idle_bank")
         for i in range(WARM_UP_MATMULS):
-            nc.tensor.matmul(idle_bank[:], zeros, zeros, start=True, stop=True)
+            nc.tensor.matmul(
+                idle_bank[:], zero[:].to_broadcast([P, P]), zero[:].to_broadcast([P, S]), start=True, stop=True
+            )
 
         identity = held.tile([P, P], BF16, name="identity")
         nc.vector.memset(identity[:], 0.0)

@@ -19,7 +19,7 @@ K_BLOCKS = K // P
 PIECE_COLUMNS = Q // 16
 ROW_START = 256
 PIECES = 2
-WARM_UP_MATMULS = 3
+WARM_UP_MATMULS = 2
 
 FLOPS = 2 * M * K * N
 

@@ -17,6 +17,9 @@ Q = N // E
 M_BLOCKS = M // P
 K_BLOCKS = K // P
 PIECE_COLUMNS = Q // 16
+BANK_BYTES = 2048
+IDLE_BANK = 2
+WINDOW_BANKS = [0, 4]
 ROW_START = 256
 PIECES = 2
 WARM_UP_MATMULS = 2
@@ -32,7 +35,7 @@ def tile_scatter_matmul_kernel(tc, base, x, w, s, b, offs, out):
     ):
         zero = held.tile([P, 1], BF16, name="zero")
         nc.gpsimd.memset(zero[:], 0.0)
-        idle_bank = banks.tile([P, S], F32, name="idle_bank")
+        idle_bank = banks.tile([P, S], F32, name="idle_bank", offset=IDLE_BANK * BANK_BYTES)
         for i in range(WARM_UP_MATMULS):
             nc.tensor.matmul(
                 idle_bank[:], zero[:].to_broadcast([P, P]), zero[:].to_broadcast([P, S]), start=True, stop=True
@@ -81,7 +84,9 @@ def tile_scatter_matmul_kernel(tc, base, x, w, s, b, offs, out):
         nc.sync.dma_start(gain[:], s.rearrange("(a p) o -> p (a o)", p=P))
         nc.sync.dma_start(shift[:], b.rearrange("(a p) o -> p (a o)", p=P))
 
-        windows = [banks.tile([P, S], F32, name=f"window{a}") for a in range(M_BLOCKS)]
+        windows = [
+            banks.tile([P, S], F32, name=f"window{a}", offset=WINDOW_BANKS[a] * BANK_BYTES) for a in range(M_BLOCKS)
+        ]
         for a in range(M_BLOCKS):
             nc.tensor.matmul(windows[a][:], identity[:], base_tiles[a][:], start=True, stop=False)
 

@@ -6,6 +6,7 @@ F32 = mybir.dt.float32
 U16 = mybir.dt.uint16
 MULT = mybir.AluOpType.mult
 ADD = mybir.AluOpType.add
+IDENTITY = mybir.ActivationFunctionType.Identity
 
 P = 128
 M = 256
@@ -40,6 +41,9 @@ def tile_scatter_matmul_kernel(tc, base, x, w, s, b, offs, out):
             nc.tensor.matmul(
                 idle_bank[:], zero[:].to_broadcast([P, P]), zero[:].to_broadcast([P, S]), start=True, stop=True
             )
+
+        primed = held.tile([P, 1], F32, name="primed")
+        nc.scalar.activation(primed[:], zero[:], IDENTITY)
 
         identity = held.tile([P, P], BF16, name="identity")
         nc.vector.memset(identity[:], 0.0)
@@ -111,12 +115,22 @@ def tile_scatter_matmul_kernel(tc, base, x, w, s, b, offs, out):
             result = held.tile([P, S], F32, name=f"result{a}", align_bytes=ROW_START)
             for i in range(PIECES):
                 columns = slice(i * (S // PIECES), (i + 1) * (S // PIECES))
-                nc.vector.tensor_scalar(
-                    result[:, columns],
-                    windows[a][:, columns],
-                    gain[:, a : a + 1],
-                    shift[:, a : a + 1],
-                    MULT,
-                    ADD,
-                )
-                nc.sync.dma_start(out[a * P : (a + 1) * P, columns], result[:, columns])
+                if a == 0:
+                    nc.scalar.activation(
+                        result[:, columns],
+                        windows[a][:, columns],
+                        IDENTITY,
+                        bias=shift[:, a : a + 1],
+                        scale=gain[:, a : a + 1],
+                    )
+                    nc.scalar.dma_start(out[a * P : (a + 1) * P, columns], result[:, columns])
+                else:
+                    nc.vector.tensor_scalar(
+                        result[:, columns],
+                        windows[a][:, columns],
+                        gain[:, a : a + 1],
+                        shift[:, a : a + 1],
+                        MULT,
+                        ADD,
+                    )
+                    nc.sync.dma_start(out[a * P : (a + 1) * P, columns], result[:, columns])

import concourse.mybir as mybir
from concourse.masks import make_identity

BF16 = mybir.dt.bfloat16
F32 = mybir.dt.float32
U16 = mybir.dt.uint16
MULT = mybir.AluOpType.mult
ADD = mybir.AluOpType.add
IDENTITY = mybir.ActivationFunctionType.Identity

P = 128
M = 256
S = 512
K = 512
N = 256
E = 2
Q = N // E
M_BLOCKS = M // P
K_BLOCKS = K // P
PIECE_COLUMNS = Q // 16
BANK_BYTES = 2048
IDLE_BANK = 2
WINDOW_BANKS = [0, 4]
ROW_START = 256
PIECES = 2
WARM_UP_MATMULS = 2

FLOPS = 2 * M * K * N


def tile_scatter_matmul_kernel(tc, base, x, w, s, b, offs, out):
    nc = tc.nc
    with (
        tc.tile_pool(name="held", bufs=1) as held,
        tc.psum_pool(name="banks", bufs=1) as banks,
    ):
        zero = held.tile([P, 1], BF16, name="zero")
        nc.gpsimd.memset(zero[:], 0.0)
        idle_bank = banks.tile([P, S], F32, name="idle_bank", offset=IDLE_BANK * BANK_BYTES)
        for i in range(WARM_UP_MATMULS):
            nc.tensor.matmul(
                idle_bank[:], zero[:].to_broadcast([P, P]), zero[:].to_broadcast([P, S]), start=True, stop=True
            )

        primed = held.tile([P, 1], F32, name="primed")
        nc.scalar.activation(primed[:], zero[:], IDENTITY)

        identity = held.tile([P, P], BF16, name="identity")
        nc.vector.memset(identity[:], 0.0)
        make_identity(nc, identity[:], nomemset=True)

        x_blocks = x.rearrange("(p c) j -> p c j", c=K_BLOCKS)
        w_blocks = w.rearrange("e (p c) m -> p e c m", c=K_BLOCKS)

        base_tiles = [
            held.tile([P, S], BF16, name=f"base_tile{a}", align_bytes=ROW_START) for a in range(M_BLOCKS)
        ]
        for a in range(M_BLOCKS):
            nc.sync.dma_start(base_tiles[a][:], base[a * P : (a + 1) * P, :])
        offsets = held.tile([P, N // 16], U16, name="offsets")
        nc.sync.dma_start(offsets[:], offs)

        x_block = {}
        w_block = {}

        def load_x(first, count):
            part = held.tile([P, count, N], BF16, name=f"x_part{first}", align_bytes=ROW_START)
            nc.sync.dma_start(part[:], x_blocks[:, first : first + count])
            for c in range(count):
                x_block[first + c] = part[:, c]

        def load_w(e, first, count):
            part = held.tile([P, count, M], BF16, name=f"w_part{e}_{first}", align_bytes=ROW_START)
            nc.sync.dma_start(part[:], w_blocks[:, e, first : first + count])
            for c in range(count):
                w_block[e, first + c] = part[:, c]

        load_x(0, 1)
        load_w(0, 0, 1)
        load_w(1, 0, 2)
        load_x(1, 1)
        load_w(0, 1, 3)
        load_x(2, 2)
        load_w(1, 2, 2)

        gain = held.tile([P, M_BLOCKS], F32, name="gain")
        shift = held.tile([P, M_BLOCKS], F32, name="shift")
        nc.sync.dma_start(gain[:], s.rearrange("(a p) o -> p (a o)", p=P))
        nc.sync.dma_start(shift[:], b.rearrange("(a p) o -> p (a o)", p=P))

        windows = [
            banks.tile([P, S], F32, name=f"window{a}", offset=WINDOW_BANKS[a] * BANK_BYTES) for a in range(M_BLOCKS)
        ]
        for a in range(M_BLOCKS):
            nc.tensor.matmul(windows[a][:], identity[:], base_tiles[a][:], start=True, stop=False)

        def scatter(a, e, c, closes):
            nc.tensor.matmul(
                windows[a][:].indirect(offsets[:, e * PIECE_COLUMNS : (e + 1) * PIECE_COLUMNS]),
                w_block[e, c][:, a * P : (a + 1) * P],
                x_block[c][:, e * Q : (e + 1) * Q],
                start=False,
                stop=closes,
            )

        for e, c in [(0, 0), (1, 0), (1, 1), (0, 1)]:
            for a in range(M_BLOCKS):
                scatter(a, e, c, closes=False)
        for a in range(M_BLOCKS):
            for e in range(E):
                for c in range(2, K_BLOCKS):
                    scatter(a, e, c, closes=(e == E - 1 and c == K_BLOCKS - 1))

        for a in range(M_BLOCKS):
            result = held.tile([P, S], F32, name=f"result{a}", align_bytes=ROW_START)
            for i in range(PIECES):
                columns = slice(i * (S // PIECES), (i + 1) * (S // PIECES))
                if a == 0:
                    nc.scalar.activation(
                        result[:, columns],
                        windows[a][:, columns],
                        IDENTITY,
                        bias=shift[:, a : a + 1],
                        scale=gain[:, a : a + 1],
                    )
                    nc.scalar.dma_start(out[a * P : (a + 1) * P, columns], result[:, columns])
                else:
                    nc.vector.tensor_scalar(
                        result[:, columns],
                        windows[a][:, columns],
                        gain[:, a : a + 1],
                        shift[:, a : a + 1],
                        MULT,
                        ADD,
                    )
                    nc.sync.dma_start(out[a * P : (a + 1) * P, columns], result[:, columns])
